import numpy as np
CORES = [3,11,19,27,35,43,51,59,67,75,83,91,131,139,147,155]
N = 16
WIDTHS = [128,128,128,12,256,256,12,128,256,256,256,256,12,12,64,256]
XW = 256
def setup_inputs(rng):
    return {"x": rng.standard_normal((N, 128, XW), dtype=np.float32)}
def reference(x):
    g = np.concatenate([x[r][:, :WIDTHS[r]] for r in range(N)], axis=1)
    return {"y": np.broadcast_to(g, (N,) + g.shape)}

from concourse.bass import DstId, RemoteDMATransfer

WIDTHS = [128, 128, 128, 12, 256, 256, 12, 128, 256, 256, 256, 256, 12, 12, 64, 256]
NPAIR = 8
SPLIT = 128
SITE = {"r": 3, "a0": 7}
FWD = {1: 2, 0: 6}
UNITS = [[0, 1], [2, 3], [4, 5], [6, 7], [8, 9], [10, 11], [12, 13, 14, 15]]
LO8, HI8 = 0x00FF, 0xFF00
STEP = 576
HB1 = 2
HD = 0
N1 = {256: 4, 128: 4}
SELF_DIE = 0


def parts_of(w):
    if w > SPLIT:
        return [(0, w // 2), (w // 2, w)]
    return [(0, w)]


def plan_of(w):
    def F(d, js):
        return [("F", d, j) for j in js]
    if w > SPLIT:
        nf = 7 - HD
        dj = [("D", j) for j in range(nf + 1, 8)]
        calls = [[(0, LO8, F(1, range(1, nf + 1))), (1, HI8, [("H", "a0")] + F(0, [0]))]]
        if HB1:
            calls.append([(1, LO8, F(1, range(1, HB1 + 1))), (0, HI8, F(1, [0]))])
        else:
            calls.append([(0, HI8, F(1, [0]))])
        if dj:
            calls.append([(0, LO8, dj)])
        return {"r": calls, "a0": [[(1, LO8, F(0, range(HB1 + 1, nf + 1)) + dj)]]}
    n1 = N1.get(w, 0)
    if n1 == 0:
        return {"r": [[(0, HI8, [("H", "a0")] + F(SELF_DIE, [0]))]], "a0": [[(0, LO8, F(0, range(1, 8)))]]}
    if n1 == 7:
        return {"r": [[(0, LO8, F(1, range(1, 8))), (0, HI8, F(SELF_DIE, [0]))]]}
    return {"r": [[(0, LO8, F(1, range(1, n1 + 1))), (0, HI8, [("H", "a0")] + F(SELF_DIE, [0]))]],
            "a0": [[(0, LO8, F(0, range(n1 + 1, 8)))]]}


def flows(widths):
    fin, due = {}, [{} for t in widths]
    for q, w in enumerate(widths):
        ps = parts_of(w)
        for site, calls in plan_of(w).items():
            now = 0 if site == "r" else STEP
            first = now
            for ci, call in enumerate(calls):
                for pi, mask, dests in call:
                    n = ps[pi][1] - ps[pi][0]
                    for de in dests:
                        if de[0] == "H":
                            continue
                        pair = (q // 2 + de[-1]) % NPAIR
                        if de[0] == "F":
                            now += n if de[2] else 0
                            t = 2 * pair + q % 2
                            at = now if de[2] else first + 32 * ci
                            fin.setdefault((t, de[1]), []).append((at, q, pi))
                            for tt in (t, t ^ 1):
                                due[tt][q] = max(due[tt].get(q, 0), at + STEP)
                        else:
                            for tt in (2 * pair + q % 2, 2 * pair + 1 - q % 2):
                                now += n
                                due[tt][q] = max(due[tt].get(q, 0), now)
    for key in fin:
        fin[key].sort()
    return fin, due


def slot_in(lst, widths, q, pi):
    def wid(a, b):
        lo, hi = parts_of(widths[a])[b]
        return hi - lo
    same = [(a, b) for e, a, b in lst if wid(a, b) == wid(q, pi)]
    return same.index((q, pi))


def classes():
    fin, due = flows(WIDTHS)
    cls = {}
    for w in WIDTHS:
        for lo, hi in parts_of(w):
            cls[hi - lo] = max(cls.get(hi - lo, 0), len(parts_of(w)))
    for lst in fin.values():
        for e, q, pi in lst:
            lo, hi = parts_of(WIDTHS[q])[pi]
            cls[hi - lo] = max(cls[hi - lo], slot_in(lst, WIDTHS, q, pi) + 1)
    return cls


SCRATCH = {"land": ("sbuf", [128, sum(WIDTHS)], "float32")}
for cn, ck in classes().items():
    SCRATCH["s%d" % cn] = ("dram", [ck, 128, cn], "float32")

SEMAPHORES = ["ld", "snt", "gd", "st"] + ["p%d_%d" % (q, i) for q in range(len(WIDTHS)) for i in range(len(parts_of(WIDTHS[q])))]


def rank_program(g, core, T, topo):
    widths = T.tables["WIDTHS"]
    local = core % 8
    base = core - local
    r = T.rank_of(base + SITE["r"])
    if r is None:
        return
    off = [sum(widths[:q]) for q in range(len(widths) + 1)]
    w = widths[r]
    sem = T.sem
    fin, due = flows(widths)

    def dst(c):
        rid, pid = topo.addr(c, core)
        return DstId(rid=rid, pnc=pid)

    def buf(q, pi):
        lo, hi = parts_of(widths[q])[pi]
        return T["s%d" % (hi - lo)]

    def psem(q, pi):
        return sem["p%d_%d" % (q, pi)]

    def cols(q, pi):
        lo, hi = parts_of(widths[q])[pi]
        return T.land[:, off[q] + lo:off[q] + hi]

    def ones(mask):
        return bin(mask).count("1")

    def fan(calls):
        total = 0
        for call in calls:
            trs = []
            for pi, mask, dests in call:
                ids, outs = [], []
                for de in dests:
                    if de[0] == "H":
                        ids.append(dst(base + SITE[de[1]]))
                        outs.append(buf(r, pi)[pi])
                        continue
                    pair = (r // 2 + de[-1]) % NPAIR
                    if de[0] == "F":
                        t = 2 * pair + r % 2
                        ids.append(dst(T.cores[t] - SITE["r"] + FWD[de[1]]))
                        outs.append(buf(r, pi)[slot_in(fin[(t, de[1])], widths, r, pi)])
                    else:
                        for t in (2 * pair + r % 2, 2 * pair + 1 - r % 2):
                            ids.append(dst(T.cores[t]))
                            outs.append(cols(r, pi))
                trs.append(RemoteDMATransfer(dst_ids=ids, dma_engine_mask=mask, remote_sem=psem(r, pi),
                                             srcs=[buf(r, pi)[pi]], dsts=outs))
                total += ones(mask)
            g.remote_dma_fused(trs, local_sem=sem.snt)
        return total

    plan = plan_of(w)

    if local == SITE["r"]:
        queues = [g.sync, g.scalar]
        ps = parts_of(w)
        for i, (lo, hi) in enumerate(ps):
            queues[i % 2].dma_start(buf(r, i)[i], T.x[:, lo:hi]).then_inc(sem.ld, 16)
        g.wait_ge(sem.ld, 16 * len(ps))
        sent = fan(plan["r"])
        g.dma_start(T.y[:, off[r]:off[r] + w], T.x[:, 0:w]).then_inc(sem.gd, 16)
        todo = []
        for ranks in UNITS:
            others = [q for q in ranks if q != r]
            if others:
                todo.append((max(due[r][q] for q in others), others))
        stores = 0
        for i, (e, others) in enumerate(sorted(todo)):
            qu = queues[i % 2]
            for q in others:
                for pi in range(len(parts_of(widths[q]))):
                    qu.wait_ge(psem(q, pi), 8)
            runs = []
            for q in others:
                if runs and runs[-1][1] == off[q]:
                    runs[-1][1] = off[q + 1]
                else:
                    runs.append([off[q], off[q + 1]])
            for a, b in runs:
                qu.dma_start(T.y[:, a:b], T.land[:, a:b]).then_inc(sem.st, 16)
                stores += 1
        g.wait_ge(sem.snt, sent)
        g.wait_ge(sem.gd, 16)
        g.wait_ge(sem.st, 16 * stores)
        return

    for site in plan:
        if site != "r" and local == SITE[site]:
            for call in plan["r"]:
                for pi, mask, dests in call:
                    if ("H", site) in dests:
                        g.wait_ge(psem(r, pi), ones(mask))
            g.wait_ge(sem.snt, fan(plan[site]))
            return

    for d in (0, 1):
        if local == FWD[d]:
            lst = fin.get((r, d), [])
            total = 0
            for e, q, pi in lst:
                src = buf(q, pi)[slot_in(lst, widths, q, pi)]
                g.wait_ge(psem(q, pi), 8)
                trs = [RemoteDMATransfer(dst_ids=[dst(T.cores[r ^ 1])], dma_engine_mask=LO8, remote_sem=psem(q, pi),
                                         src=src, dst=cols(q, pi))]
                total += 8
                if q != r:
                    trs.append(RemoteDMATransfer(dst_ids=[dst(base + SITE["r"])], dma_engine_mask=HI8,
                                                 remote_sem=psem(q, pi), src=src, dst=cols(q, pi)))
                    total += 8
                g.remote_dma_fused(trs, local_sem=sem.snt)
            if total:
                g.wait_ge(sem.snt, total)
            return
